import numpy as np
import ml_dtypes


def mxq(x, axis, fmt="e4m3"):
    dtype, down = {"e4m3": (ml_dtypes.float8_e4m3fn, 7), "e5m2": (ml_dtypes.float8_e5m2, 14)}[fmt]
    v = np.moveaxis(np.asarray(x, np.float32).astype(ml_dtypes.bfloat16).astype(np.float64), axis, -1)
    blocks = v.reshape(v.shape[:-1] + (-1, 32))
    amax = np.abs(blocks).max(-1, keepdims=True)
    byte = np.maximum(np.where(amax > 0, np.frexp(amax)[1] - 1 + 127, 0) - down, 1)
    scale = np.exp2(byte - 127.0)
    codes = (blocks / scale).astype(np.float32).astype(dtype).astype(np.float64)
    return np.moveaxis((codes * scale).reshape(v.shape), -1, axis)


WIDE = False


def mx_kscale(k):
    if not WIDE:
        return np.ones(k)
    levels = np.array([10, -10, 5, -5, 0])
    if k % 512:
        return np.exp2(np.random.permutation(np.resize(levels, k // 32))).repeat(32)
    a = np.empty((k // 512, 16))
    for p in range(k // 512):
        a[p, :8] = np.random.permutation(np.resize(levels, 8))
        for g in range(8):
            far = levels[np.abs(levels - a[p, g]) >= 10]
            a[p, g + 8] = far[np.random.randint(len(far))]
    return np.exp2(a.ravel()).repeat(32)


def f64(x):
    return np.asarray(x).astype(np.float64)


def striped(idx):
    return np.tile(idx.reshape(-1, 16).T, (8, 1)).astype(np.uint16)


def unstriped(offs):
    return offs[:16].T.reshape(-1).astype(np.int64)


E2M1 = np.array([0.0, 0.5, 1.0, 1.5, 2.0, 3.0, 4.0, 6.0, -0.0, -0.5, -1.0, -1.5, -2.0, -3.0, -4.0, -6.0])


def pack_weight(w, fmt):
    k, n = w.shape
    w = f64(np.asarray(w, np.float32).astype(ml_dtypes.bfloat16)).reshape(k // 32, 32, n)
    amax = np.abs(w).max(1)
    if fmt == "e4m3":
        byte = np.frexp(amax)[1] - 1 + 127 - 7
    else:
        mant, ex = np.frexp(amax / 6.0)
        byte = np.where(mant > 0.5, ex, ex - 1) + 127
    byte = np.clip(np.where(amax > 0, byte, 1), 1, 254)
    scaled = (w * np.exp2(127.0 - byte)[:, None, :]).reshape(k, n).astype(np.float32)
    by_word = np.ascontiguousarray(scaled.reshape(k // 512, 128, 4, n).transpose(0, 1, 3, 2))
    if fmt == "e4m3":
        words = by_word.astype(ml_dtypes.float8_e4m3fn).view(np.uint8)
    else:
        c = by_word.astype(ml_dtypes.float4_e2m1fn).view(np.uint8) & 0xF
        words = (c[..., 0::2] | (c[..., 1::2] << 4)).reshape(k // 512, 128, 2 * n)
    return np.ascontiguousarray(words), np.ascontiguousarray(byte.astype(np.uint8).reshape(k // 512, 16, n))


def unpack_weight(words, scales, fmt):
    g, _, n = scales.shape
    words = np.ascontiguousarray(words).reshape(g, 128, n, -1)
    if fmt == "e4m3":
        vals = words.view(ml_dtypes.float8_e4m3fn).astype(np.float64)
    else:
        nib = np.empty((g, 128, n, 4), np.uint8)
        nib[..., 0::2] = words & 0xF
        nib[..., 1::2] = words >> 4
        vals = E2M1[nib]
    vals = vals * np.repeat(np.exp2(scales.astype(np.float64) - 127.0), 8, axis=1)[..., None]
    return vals.transpose(0, 1, 3, 2).reshape(g * 512, n)


def gelu(v):
    return 0.5 * v * (1.0 + np.tanh(np.sqrt(2.0 / np.pi) * (v + 0.044715 * v**3)))


def striped8(idx):
    return np.concatenate([v.reshape(-1, 16).T for v in idx]).astype(np.uint16)


def unstriped8(offs):
    return np.stack([offs[16 * g:16 * g + 16].T.reshape(-1) for g in range(8)]).astype(np.int64)


def heads(h, wgt, idx8):
    r = np.arange(h.shape[0])
    return wgt[r // 4 % 128] * h[r[:, None], idx8[r % 512 // 64]]


K, T, S, H, T2, P, N = 1536, 2048, 512, 1024, 1024, 512, 512

def setup_inputs():
    n = np.random.standard_normal
    s = mx_kscale(K)[:, None]
    u = mx_kscale(H)[:, None]
    tab_words, tab_scales = pack_weight(n((K, T)) * s, "e4m3")
    w2_words, w2_scales = pack_weight(n((H, N)) / np.sqrt(H) / u, "e2m1")
    return {
        "tab_words": tab_words, "tab_scales": tab_scales,
        "offs": striped(np.random.permutation(T)[:S]),
        "offs2": striped(np.random.permutation(T2)[:S]),
        "offs3": striped8(np.stack([np.random.permutation(T2)[:P] for _ in range(8)])),
        "w1": (1.3 * n((K, H)) / np.sqrt(K) / s).astype(np.float32),
        "b1": (0.6 * n(H)).astype(np.float32),
        "gain": (np.exp(0.3 * n(H)) * u[:, 0]).astype(np.float32),
        "wgs": np.exp(0.3 * n((128, S))).astype(np.float32),
        "page0": (n((H, T2)) * u).astype(np.float32),
        "wgt": np.repeat(np.random.uniform(0.5, 2.0, (8, P)), 16, axis=0).astype(np.float32),
        "att": n((H, P)).astype(np.float32),
        "w2_words": w2_words, "w2_scales": w2_scales,
        "w3": (n((H, N)) / np.sqrt(H) / u).astype(np.float32),
    }

def reference(tab_words, tab_scales, offs, offs2, offs3, w1, b1, gain, wgs, page0, wgt, att, w2_words, w2_scales, w3):
    v = unpack_weight(tab_words, tab_scales, "e4m3")[:, unstriped(offs)]
    y = mxq(f64(w1), 0, "e4m3").T @ v
    h = f64(gain)[:, None] * np.tanh(y + f64(b1)[:, None])
    page = f64(page0).copy()
    page[:, unstriped(offs2)] = np.tile(f64(wgs), (H // 128, 1)) * h
    x = heads(page, f64(wgt), unstriped8(offs3))
    tilt = f64(att) * x
    xq = mxq(x, 0, "e4m3")
    tq = mxq(tilt, 0, "e4m3")
    w2 = unpack_weight(w2_words, w2_scales, "e2m1")
    return w2.T @ xq + mxq(f64(w3), 0, "e4m3").T @ tq

@@ -1,0 +1,261 @@
+from contextlib import ExitStack
+
+import concourse.mybir as mybir
+
+K, T, S, H, T2, M, N = 1536, 2048, 512, 1024, 1024, 512, 512
+FLOPS = 2 * K * H * S + 2 * 2 * H * N * M
+
+F32 = mybir.dt.float32
+BF16 = mybir.dt.bfloat16
+I32 = mybir.dt.int32
+U32 = mybir.dt.uint32
+U16 = mybir.dt.uint16
+U8 = mybir.dt.uint8
+FP8X4 = mybir.dt.float8_e4m3fn_x4
+FP4X4 = mybir.dt.float4_e2m1fn_x4
+MULT = mybir.AluOpType.mult
+ACT = mybir.ActivationFunctionType
+
+P = 128
+PACK = 4
+PASS = P * PACK
+K_PASSES = K // PASS
+H_PASSES = H // PASS
+QUADS = 4
+HALF = M // 2
+
+
+def tile_list_tank_bay_gauging_kernel(
+    tc, tab_words, tab_scales, offs, offs2, offs3, w1, b1, gain, wgs, page0, wgt, att, w2_words, w2_scales, w3, out
+):
+    nc = tc.nc
+    with ExitStack() as ctx:
+        keep = ctx.enter_context(tc.tile_pool(name="keep", bufs=1))
+        raw_pool = ctx.enter_context(tc.tile_pool(name="raw", bufs=5))
+        bf_pool = ctx.enter_context(tc.tile_pool(name="bf", bufs=4))
+        h_pool = ctx.enter_context(tc.tile_pool(name="h", bufs=4))
+        psum = ctx.enter_context(tc.psum_pool(name="psum", bufs=1))
+
+        idx = keep.tile([P, S // 16], U16, name="idx")
+        idx2 = keep.tile([P, S // 16], U16, name="idx2")
+        idx3 = keep.tile([P, M // 16], U16, name="idx3")
+        tab_sc = keep.tile([P, T], U8, name="tab_sc", align_bytes=64)
+        w2_sc = keep.tile([P, H_PASSES, N], U8, name="w2_sc", align_bytes=64)
+        w2_wd = keep.tile([P, H_PASSES, 2 * N], U8, name="w2_wd", align_bytes=64)
+        bias = keep.tile([P, H_PASSES, 2 * PACK], F32, name="bias")
+        gn = keep.tile([P, H_PASSES, 2 * PACK], F32, name="gn")
+        wgs_first = keep.tile([P, S], F32, name="wgs_first")
+        wgs_rest = keep.tile([P, PACK - 1, S], F32, name="wgs_rest")
+        wgt_sb = keep.tile([P, M], F32, name="wgt_sb")
+        tab_wd = [keep.tile([P, T], I32, name="tab_wd%d" % a, align_bytes=64) for a in range(K_PASSES)]
+        v_wd = [keep.tile([P, S], U32, name="v_wd%d" % a, align_bytes=64) for a in range(K_PASSES)]
+        v_sc = keep.tile([P, S], U8, name="v_sc", align_bytes=64)
+        page = [[keep.tile([P, T2], F32, name="page%d_%d" % (b, i)) for i in range(PACK)] for b in range(H_PASSES)]
+        att_sb = [keep.tile([P, PACK, M], F32, name="att%d" % b) for b in range(H_PASSES)]
+        y_bank = [psum.tile([P, S], F32, name="y%d" % i) for i in range(PACK)]
+        out_bank = [[psum.tile([P, 2, HALF], F32, name="o%d_%d" % (hf, g)) for g in range(2)] for hf in range(2)]
+
+        page_rows = page0.rearrange("(b p i) t -> b i p t", p=P, i=PACK)
+        wgs_rows = wgs.rearrange("(q i) j -> q i j", i=PACK)
+
+        def load_rows(w, a, cols):
+            raw = raw_pool.tile([P, PACK, PASS], F32, name="raw")
+            nc.sync.dma_start(out=raw[:], in_=w[a * PASS:(a + 1) * PASS, cols].rearrange("(p j) c -> p j c", j=PACK))
+            return raw
+
+        def load_table(a):
+            nc.sync.dma_start(out=tab_wd[a][:], in_=tab_words[a].rearrange("p t i -> p (t i)").bitcast(I32))
+
+        def load_page(b, i):
+            nc.sync.dma_start(out=page[b][i][:], in_=page_rows[b, i])
+
+        def load_att(b):
+            nc.sync.dma_start(out=att_sb[b][:], in_=att[b * PASS:(b + 1) * PASS, :].rearrange("(p i) m -> p i m", i=PACK))
+
+        def quantise(grouped, width, name):
+            codes = keep.tile([P, width], U32, name=name + "_wd", align_bytes=64)
+            scales = keep.tile([P, width], U8, name=name + "_sc", align_bytes=64)
+            nc.vector.quantize_mx(out=codes[:].bitcast(FP8X4), scales=scales[:], in_=grouped)
+            return codes, scales
+
+        def quantise_w1(raw, name):
+            grouped = bf_pool.tile([P, PACK * PASS], BF16, name="grouped", align_bytes=64)
+            nc.scalar.copy(
+                out=grouped[:].rearrange("p (t m j) -> p m j t", t=PACK, j=PACK),
+                in_=raw[:].rearrange("p j (m t) -> p m j t", t=PACK),
+            )
+            return quantise(grouped[:], PASS, name)
+
+        def interleaved(tile, width):
+            return tile[:, 0:PACK * width].rearrange("p (c i t) -> p c t i", i=4, t=PACK)
+
+        def by_runs(ap):
+            return ap.rearrange("p t (c i) -> p c t i", i=4)
+
+        def quantise_w3(raw, name):
+            grouped = bf_pool.tile([P, PACK * PASS], BF16, name="grouped", align_bytes=64)
+            nc.scalar.copy(out=interleaved(grouped, N), in_=by_runs(raw[:]))
+            return quantise(grouped[:], N, name)
+
+        def gather_table(a):
+            nc.vector.tensor_copy(out=v_wd[a][:], in_=tab_wd[a][:].bitcast(U32).indirect(idx[:]))
+
+        def first_product(a, w1q):
+            codes, scales = w1q
+            for i in range(PACK):
+                cols = slice(i * P, (i + 1) * P)
+                nc.tensor.matmul_mx(
+                    out=y_bank[i][:],
+                    lhsT=codes[:, cols].bitcast(FP8X4), lhsT_scale=scales[:, cols],
+                    rhs=v_wd[a][:].bitcast(FP8X4), rhs_scale=v_sc[4 * a:P, :],
+                    start=(a == 0), stop=(a == K_PASSES - 1),
+                )
+
+        def features(b, i):
+            th = h_pool.tile([P, S], F32, name="th")
+            nc.scalar.activation(out=th[:], in_=y_bank[i][:], func=ACT.Tanh, bias=bias[:, b, i:i + 1])
+            h = h_pool.tile([P, S], F32, name="h")
+            nc.scalar.activation(out=h[:], in_=th[:], func=ACT.Copy, scale=gn[:, b, i:i + 1])
+            return h
+
+        def scatter(b, i, h):
+            w_row = wgs_first[:] if i == 0 else wgs_rest[:, i - 1, :]
+            nc.vector.tensor_tensor(out=page[b][i][:].indirect(idx2[:]), in0=h[:], in1=w_row, op=MULT)
+
+        def gather(b, i, x, m0, width):
+            offsets = idx3[:, m0 // 16:(m0 + width) // 16]
+            nc.vector.tensor_tensor(out=x[:, i, :], in0=page[b][i][:].indirect(offsets), in1=wgt_sb[:, m0:m0 + width], op=MULT)
+
+        def round_x(x, width):
+            grouped = bf_pool.tile([P, PACK * PASS], BF16, name="grouped", align_bytes=64)
+            nc.scalar.copy(out=interleaved(grouped, width), in_=by_runs(x[:]))
+            return grouped[:, 0:PACK * width]
+
+        def make_tilt(b, x, m0, width):
+            grouped = bf_pool.tile([P, PACK * PASS], BF16, name="grouped", align_bytes=64)
+            nc.vector.tensor_tensor(
+                out=interleaved(grouped, width), in0=by_runs(x[:]), in1=by_runs(att_sb[b][:, :, m0:m0 + width]), op=MULT
+            )
+            return grouped[:, 0:PACK * width]
+
+        def second_product(b, hf, with_w2, moving, c0, w3q):
+            codes, scales = moving
+            cols = slice(c0, c0 + HALF)
+            for nt in range(N // P):
+                n_cols = slice(nt * P, (nt + 1) * P)
+                if with_w2:
+                    lhsT = w2_wd[:, b, 2 * nt * P:2 * (nt + 1) * P].bitcast(FP4X4)
+                    lhsT_scale = w2_sc[:, b, n_cols]
+                else:
+                    lhsT = w3q[0][:, n_cols].bitcast(FP8X4)
+                    lhsT_scale = w3q[1][:, n_cols]
+                nc.tensor.matmul_mx(
+                    out=out_bank[hf][nt // 2][:, nt % 2, :],
+                    lhsT=lhsT, lhsT_scale=lhsT_scale,
+                    rhs=codes[:, cols].bitcast(FP8X4), rhs_scale=scales[:, cols],
+                    start=(b == 0 and with_w2 and nt % 2 == 0),
+                    stop=(b == H_PASSES - 1 and not with_w2 and nt % 2 == 1),
+                )
+
+        def store(hf, g, on_vector):
+            res = keep.tile([P, 2, HALF], F32, name="res%d_%d" % (hf, g))
+            if on_vector:
+                nc.vector.tensor_copy(out=res[:], in_=out_bank[hf][g][:])
+            else:
+                nc.scalar.copy(out=res[:], in_=out_bank[hf][g][:])
+            rows = out[2 * g * P:2 * (g + 1) * P, hf * HALF:(hf + 1) * HALF]
+            nc.sync.dma_start(out=rows.rearrange("(u p) m -> p u m", p=P), in_=res[:])
+
+        half0 = slice(0, PASS)
+        half1 = slice(PASS, 2 * PASS)
+        nc.gpsimd.memset(tab_sc[:].bitcast(I32), 0)
+        nc.gpsimd.memset(w2_sc[:].bitcast(I32), 0)
+        nc.sync.dma_start(out=idx[:], in_=offs)
+        raw0 = [load_rows(w1, 0, half0)]
+        for q in range(QUADS):
+            nc.sync.dma_start(
+                out=tab_sc[32 * q:32 * q + 4 * K_PASSES, :].bitcast(I32),
+                in_=tab_scales[:, 4 * q:4 * q + 4, :].bitcast(I32),
+            )
+        raw0.extend([load_rows(w1, a, half0) for a in range(1, K_PASSES)])
+        load_table(0)
+        nc.sync.dma_start(out=bias[:, :, 0:PACK], in_=b1.rearrange("(b p i) -> p b i", p=P, i=PACK))
+        nc.sync.dma_start(out=gn[:, :, 0:PACK], in_=gain.rearrange("(b p i) -> p b i", p=P, i=PACK))
+        load_table(1)
+        nc.sync.dma_start(out=idx2[:], in_=offs2)
+        nc.sync.dma_start(out=idx3[:], in_=offs3)
+        load_table(2)
+        load_page(0, 0)
+        for q in range(QUADS):
+            nc.sync.dma_start(out=wgs_first[32 * q:32 * (q + 1), :], in_=wgs_rows[:, 0, :])
+        load_page(0, 1)
+        for q in range(QUADS):
+            nc.sync.dma_start(out=wgs_rest[32 * q:32 * (q + 1), :, :], in_=wgs_rows[:, 1:PACK, :])
+        nc.sync.dma_start(out=wgt_sb[:], in_=wgt)
+        raw1 = [load_rows(w1, 0, half1)]
+        load_page(0, 2)
+        raw1.extend([load_rows(w1, a, half1) for a in range(1, K_PASSES)])
+        load_page(0, 3)
+        load_att(0)
+        load_page(1, 0)
+        nc.sync.dma_start(out=w2_wd[:].bitcast(I32), in_=w2_words.rearrange("a p c -> p a c").bitcast(I32))
+        for q in range(QUADS):
+            nc.sync.dma_start(
+                out=w2_sc[32 * q:32 * q + 4, :, :].bitcast(I32),
+                in_=w2_scales[:, 4 * q:4 * q + 4, :].rearrange("a r n -> r a n").bitcast(I32),
+            )
+
+        nc.vector.tensor_copy(out=v_sc[:], in_=tab_sc[:].indirect(idx[:]))
+        w1q = [quantise_w1(raw0[a], "w1q0_%d" % a) for a in range(K_PASSES)]
+        for a in range(K_PASSES):
+            gather_table(a)
+            first_product(a, w1q[a])
+        raw3 = [load_rows(w3, 0, slice(0, N))]
+        load_page(1, 1)
+        raw3.append(load_rows(w3, 1, slice(0, N)))
+        load_page(1, 2)
+        load_att(1)
+        load_page(1, 3)
+        h0 = [features(0, i) for i in range(PACK)]
+        x0 = keep.tile([P, PACK, M], F32, name="x0")
+        scatter(0, 0, h0[0])
+        for i in range(PACK):
+            if i + 1 < PACK:
+                scatter(0, i + 1, h0[i + 1])
+            gather(0, i, x0, 0, M)
+
+        for a in range(K_PASSES):
+            first_product(a, quantise_w1(raw1[a], "w1q1_%d" % a))
+
+        x0_bf = round_x(x0, M)
+        tilt0_bf = make_tilt(0, x0, 0, M)
+        h1 = [features(1, i) for i in range(PACK)]
+        xq0 = quantise(x0_bf, M, "xq0")
+        tq0 = quantise(tilt0_bf, M, "tq0")
+        w3q = [quantise_w3(raw3[b], "w3q%d" % b) for b in range(H_PASSES)]
+        for hf in range(2):
+            second_product(0, hf, True, xq0, hf * HALF, None)
+        for hf in range(2):
+            second_product(0, hf, False, tq0, hf * HALF, w3q[0])
+
+        x1 = [keep.tile([P, PACK, HALF], F32, name="x1_%d" % hf) for hf in range(2)]
+        scatter(1, 0, h1[0])
+        for i in range(PACK):
+            if i + 1 < PACK:
+                scatter(1, i + 1, h1[i + 1])
+            gather(1, i, x1[0], 0, HALF)
+        for hf in range(2):
+            if hf == 0:
+                x_bf = round_x(x1[0], HALF)
+                tilt_bf = make_tilt(1, x1[0], 0, HALF)
+                for i in range(PACK):
+                    gather(1, i, x1[1], HALF, HALF)
+            else:
+                x_bf = round_x(x1[1], HALF)
+                tilt_bf = make_tilt(1, x1[1], HALF, HALF)
+            xq = quantise(x_bf, HALF, "xq1_%d" % hf)
+            second_product(1, hf, True, xq, 0, None)
+            tq = quantise(tilt_bf, HALF, "tq1_%d" % hf)
+            second_product(1, hf, False, tq, 0, w3q[1])
+            for g in range(2):
+                store(hf, g, hf == 1 and g == 1)

@@ -1,6 +1,7 @@
 from contextlib import ExitStack
 
 import concourse.mybir as mybir
+from concourse.masks import make_identity
 
 K, T, S, H, T2, M, N = 1536, 2048, 512, 1024, 1024, 512, 512
 FLOPS = 2 * K * H * S + 2 * 2 * H * N * M
@@ -32,8 +33,8 @@ def tile_list_tank_bay_gauging_kernel(
     with ExitStack() as ctx:
         keep = ctx.enter_context(tc.tile_pool(name="keep", bufs=1))
         raw_pool = ctx.enter_context(tc.tile_pool(name="raw", bufs=5))
-        bf_pool = ctx.enter_context(tc.tile_pool(name="bf", bufs=4))
-        h_pool = ctx.enter_context(tc.tile_pool(name="h", bufs=4))
+        bf_pool = ctx.enter_context(tc.tile_pool(name="bf", bufs=5))
+        h_pool = ctx.enter_context(tc.tile_pool(name="h", bufs=6))
         psum = ctx.enter_context(tc.psum_pool(name="psum", bufs=1))
 
         idx = keep.tile([P, S // 16], U16, name="idx")
@@ -44,8 +45,8 @@ def tile_list_tank_bay_gauging_kernel(
         w2_wd = keep.tile([P, H_PASSES, 2 * N], U8, name="w2_wd", align_bytes=64)
         bias = keep.tile([P, H_PASSES, 2 * PACK], F32, name="bias")
         gn = keep.tile([P, H_PASSES, 2 * PACK], F32, name="gn")
-        wgs_first = keep.tile([P, S], F32, name="wgs_first")
-        wgs_rest = keep.tile([P, PACK - 1, S], F32, name="wgs_rest")
+        wgs_sb = keep.tile([P, S], F32, name="wgs_sb")
+        ident = keep.tile([P, P], F32, name="ident")
         wgt_sb = keep.tile([P, M], F32, name="wgt_sb")
         tab_wd = [keep.tile([P, T], I32, name="tab_wd%d" % a, align_bytes=64) for a in range(K_PASSES)]
         v_wd = [keep.tile([P, S], U32, name="v_wd%d" % a, align_bytes=64) for a in range(K_PASSES)]
@@ -56,10 +57,9 @@ def tile_list_tank_bay_gauging_kernel(
         out_bank = [[psum.tile([P, 2, HALF], F32, name="o%d_%d" % (hf, g)) for g in range(2)] for hf in range(2)]
 
         page_rows = page0.rearrange("(b p i) t -> b i p t", p=P, i=PACK)
-        wgs_rows = wgs.rearrange("(q i) j -> q i j", i=PACK)
 
         def load_rows(w, a, cols):
-            raw = raw_pool.tile([P, PACK, PASS], F32, name="raw")
+            raw = raw_pool.tile([P, PACK, PASS], F32, name="raw", tag="raw")
             nc.sync.dma_start(out=raw[:], in_=w[a * PASS:(a + 1) * PASS, cols].rearrange("(p j) c -> p j c", j=PACK))
             return raw
 
@@ -97,30 +97,54 @@ def tile_list_tank_bay_gauging_kernel(
             nc.scalar.copy(out=interleaved(grouped, N), in_=by_runs(raw[:]))
             return quantise(grouped[:], N, name)
 
-        def gather_table(a):
-            nc.vector.tensor_copy(out=v_wd[a][:], in_=tab_wd[a][:].bitcast(U32).indirect(idx[:]))
+        def gather_table(a, j0, width):
+            nc.vector.tensor_copy(
+                out=v_wd[a][:, j0:j0 + width], in_=tab_wd[a][:].bitcast(U32).indirect(idx[:, j0 // 16:(j0 + width) // 16])
+            )
 
-        def first_product(a, w1q):
+        def first_pass(bank, a, w1q, i, j0, width):
             codes, scales = w1q
-            for i in range(PACK):
-                cols = slice(i * P, (i + 1) * P)
-                nc.tensor.matmul_mx(
-                    out=y_bank[i][:],
-                    lhsT=codes[:, cols].bitcast(FP8X4), lhsT_scale=scales[:, cols],
-                    rhs=v_wd[a][:].bitcast(FP8X4), rhs_scale=v_sc[4 * a:P, :],
-                    start=(a == 0), stop=(a == K_PASSES - 1),
-                )
+            cols = slice(i * P, (i + 1) * P)
+            nc.tensor.matmul_mx(
+                out=bank[:, 0:width],
+                lhsT=codes[:, cols].bitcast(FP8X4), lhsT_scale=scales[:, cols],
+                rhs=v_wd[a][:, j0:j0 + width].bitcast(FP8X4), rhs_scale=v_sc[4 * a:P, j0:j0 + width],
+                start=(a == 0), stop=(a == K_PASSES - 1),
+            )
 
-        def features(b, i):
+        def tanh(b, i, bank, width):
             th = h_pool.tile([P, S], F32, name="th")
-            nc.scalar.activation(out=th[:], in_=y_bank[i][:], func=ACT.Tanh, bias=bias[:, b, i:i + 1])
-            h = h_pool.tile([P, S], F32, name="h")
-            nc.scalar.activation(out=h[:], in_=th[:], func=ACT.Copy, scale=gn[:, b, i:i + 1])
-            return h
+            nc.scalar.activation(out=th[:, 0:width], in_=bank[:, 0:width], func=ACT.Tanh, bias=bias[:, b, i:i + 1])
+            return th[:, 0:width]
 
-        def scatter(b, i, h):
-            w_row = wgs_first[:] if i == 0 else wgs_rest[:, i - 1, :]
-            nc.vector.tensor_tensor(out=page[b][i][:].indirect(idx2[:]), in0=h[:], in1=w_row, op=MULT)
+        def scatter(b, i, th, j0, width):
+            nc.vector.tensor_tensor(
+                out=page[b][i][:].indirect(idx2[:, j0 // 16:(j0 + width) // 16]),
+                in0=th, in1=wg[b][:, i, j0:j0 + width], op=MULT,
+            )
+
+        def scale_wgs(b, scaled):
+            for i in range(PACK):
+                nc.scalar.activation(out=scaled[:, i, :], in_=wgs_bank(i), func=ACT.Copy, scale=gn[:, b, i:i + 1])
+            return scaled
+
+        def wgs_bank(i):
+            return out_bank[i // 2][i % 2][:].rearrange("p u m -> p (u m)")
+
+        def deal_wgs():
+            turned = y_bank[PACK - 1]
+            for jb in range(S // P):
+                nc.tensor.transpose(out=turned[:, jb * P:(jb + 1) * P], in_=wgs_sb[:, jb * P:(jb + 1) * P], identity=ident[:])
+            dealt = raw_pool.tile([P, PACK, PASS], F32, name="dealt", tag="raw")
+            parts = dealt[:].rearrange("p jb (i r q) -> p jb i r q", i=PACK, r=QUADS)
+            nc.vector.tensor_copy(out=parts[:, :, :, 0, :], in_=turned[:].rearrange("p (jb q i) -> p jb i q", jb=S // P, i=PACK))
+            nc.vector.tensor_copy(out=parts[:, :, :, 1, :], in_=parts[:, :, :, 0, :])
+            nc.vector.tensor_copy(out=parts[:, :, :, 2:4, :], in_=parts[:, :, :, 0:2, :])
+            for i in range(PACK):
+                for jb in range(S // P):
+                    nc.tensor.transpose(
+                        out=wgs_bank(i)[:, jb * P:(jb + 1) * P], in_=dealt[:, jb, i * P:(i + 1) * P], identity=ident[:]
+                    )
 
         def gather(b, i, x, m0, width):
             offsets = idx3[:, m0 // 16:(m0 + width) // 16]
@@ -128,13 +152,13 @@ def tile_list_tank_bay_gauging_kernel(
 
         def round_x(x, width):
             grouped = bf_pool.tile([P, PACK * PASS], BF16, name="grouped", align_bytes=64)
-            nc.scalar.copy(out=interleaved(grouped, width), in_=by_runs(x[:]))
+            nc.scalar.copy(out=interleaved(grouped, width), in_=by_runs(x))
             return grouped[:, 0:PACK * width]
 
         def make_tilt(b, x, m0, width):
             grouped = bf_pool.tile([P, PACK * PASS], BF16, name="grouped", align_bytes=64)
             nc.vector.tensor_tensor(
-                out=interleaved(grouped, width), in0=by_runs(x[:]), in1=by_runs(att_sb[b][:, :, m0:m0 + width]), op=MULT
+                out=interleaved(grouped, width), in0=by_runs(x), in1=by_runs(att_sb[b][:, :, m0:m0 + width]), op=MULT
             )
             return grouped[:, 0:PACK * width]
 
@@ -168,36 +192,42 @@ def tile_list_tank_bay_gauging_kernel(
 
         half0 = slice(0, PASS)
         half1 = slice(PASS, 2 * PASS)
-        nc.gpsimd.memset(tab_sc[:].bitcast(I32), 0)
-        nc.gpsimd.memset(w2_sc[:].bitcast(I32), 0)
-        nc.sync.dma_start(out=idx[:], in_=offs)
-        raw0 = [load_rows(w1, 0, half0)]
-        for q in range(QUADS):
+
+        def load_table_scales(q):
             nc.sync.dma_start(
                 out=tab_sc[32 * q:32 * q + 4 * K_PASSES, :].bitcast(I32),
                 in_=tab_scales[:, 4 * q:4 * q + 4, :].bitcast(I32),
             )
-        raw0.extend([load_rows(w1, a, half0) for a in range(1, K_PASSES)])
-        load_table(0)
-        nc.sync.dma_start(out=bias[:, :, 0:PACK], in_=b1.rearrange("(b p i) -> p b i", p=P, i=PACK))
+
+        nc.gpsimd.memset(tab_sc[:].bitcast(I32), 0)
+        make_identity(nc, ident[:])
+        nc.gpsimd.memset(w2_sc[:].bitcast(I32), 0)
+        raw0 = [load_rows(w1, 0, half0)]
+        nc.sync.dma_start(out=wgs_sb[:], in_=wgs)
+        raw0.append(load_rows(w1, 1, half0))
         nc.sync.dma_start(out=gn[:, :, 0:PACK], in_=gain.rearrange("(b p i) -> p b i", p=P, i=PACK))
+        raw0.append(load_rows(w1, 2, half0))
+        load_table(0)
+        for q in range(QUADS):
+            load_table_scales(q)
+        nc.sync.dma_start(out=idx[:], in_=offs)
         load_table(1)
-        nc.sync.dma_start(out=idx2[:], in_=offs2)
-        nc.sync.dma_start(out=idx3[:], in_=offs3)
         load_table(2)
-        load_page(0, 0)
-        for q in range(QUADS):
-            nc.sync.dma_start(out=wgs_first[32 * q:32 * (q + 1), :], in_=wgs_rows[:, 0, :])
-        load_page(0, 1)
-        for q in range(QUADS):
-            nc.sync.dma_start(out=wgs_rest[32 * q:32 * (q + 1), :, :], in_=wgs_rows[:, 1:PACK, :])
+        nc.sync.dma_start(out=bias[:, :, 0:PACK], in_=b1.rearrange("(b p i) -> p b i", p=P, i=PACK))
+        nc.sync.dma_start(out=idx2[:], in_=offs2)
+        for i in range(PACK):
+            load_page(0, i)
+        nc.sync.dma_start(out=idx3[:], in_=offs3)
+        deal_wgs()
+        raw1 = [load_rows(w1, a, half1) for a in range(K_PASSES - 1)]
+        raw1_last = keep.tile([P, PACK, PASS], F32, name="raw1_last", tag="middle")
+        nc.sync.dma_start(out=raw1_last[:], in_=w1[(K_PASSES - 1) * PASS:K, half1].rearrange("(p j) c -> p j c", j=PACK))
+        raw1.append(raw1_last)
         nc.sync.dma_start(out=wgt_sb[:], in_=wgt)
-        raw1 = [load_rows(w1, 0, half1)]
-        load_page(0, 2)
-        raw1.extend([load_rows(w1, a, half1) for a in range(1, K_PASSES)])
-        load_page(0, 3)
-        load_att(0)
         load_page(1, 0)
+        load_att(0)
+        for i in range(1, PACK):
+            load_page(1, i)
         nc.sync.dma_start(out=w2_wd[:].bitcast(I32), in_=w2_words.rearrange("a p c -> p a c").bitcast(I32))
         for q in range(QUADS):
             nc.sync.dma_start(
@@ -207,55 +237,76 @@ def tile_list_tank_bay_gauging_kernel(
 
         nc.vector.tensor_copy(out=v_sc[:], in_=tab_sc[:].indirect(idx[:]))
         w1q = [quantise_w1(raw0[a], "w1q0_%d" % a) for a in range(K_PASSES)]
+        wg = [scale_wgs(0, keep.tile([P, PACK, S], F32, name="wg0"))]
+        last = K_PASSES - 1
+        for a in range(last):
+            gather_table(a, 0, S)
+            for hs in range(2):
+                first_pass(y_bank[hs], a, w1q[a], 0, hs * S // 2, S // 2)
+            for i in (1, 2):
+                first_pass(y_bank[i + 1], a, w1q[a], i, 0, S)
+        th00 = []
+        for hs in range(2):
+            gather_table(last, hs * S // 2, S // 2)
+            first_pass(y_bank[hs], last, w1q[last], 0, hs * S // 2, S // 2)
+            th00.append(tanh(0, 0, y_bank[hs], S // 2))
+        th0 = [None]
+        for i in (1, 2):
+            first_pass(y_bank[i + 1], last, w1q[last], i, 0, S)
+            th0.append(tanh(0, i, y_bank[i + 1], S))
         for a in range(K_PASSES):
-            gather_table(a)
-            first_product(a, w1q[a])
+            first_pass(y_bank[0], a, w1q[a], 3, 0, S)
+        th0.append(tanh(0, 3, y_bank[0], S))
         raw3 = [load_rows(w3, 0, slice(0, N))]
-        load_page(1, 1)
-        raw3.append(load_rows(w3, 1, slice(0, N)))
-        load_page(1, 2)
         load_att(1)
-        load_page(1, 3)
-        h0 = [features(0, i) for i in range(PACK)]
+        raw3_last = keep.tile([P, PACK, PASS], F32, name="raw3_last", tag="late")
+        nc.sync.dma_start(out=raw3_last[:], in_=w3[PASS:2 * PASS, :].rearrange("(p j) c -> p j c", j=PACK))
+        raw3.append(raw3_last)
         x0 = keep.tile([P, PACK, M], F32, name="x0")
-        scatter(0, 0, h0[0])
-        for i in range(PACK):
-            if i + 1 < PACK:
-                scatter(0, i + 1, h0[i + 1])
-            gather(0, i, x0, 0, M)
+        for hs in range(2):
+            scatter(0, 0, th00[hs], hs * S // 2, S // 2)
+        for i in range(1, PACK):
+            scatter(0, i, th0[i], 0, S)
 
+        banks1 = [y_bank[(i + 1) % PACK] for i in range(PACK)]
         for a in range(K_PASSES):
-            first_product(a, quantise_w1(raw1[a], "w1q1_%d" % a))
-
-        x0_bf = round_x(x0, M)
-        tilt0_bf = make_tilt(0, x0, 0, M)
-        h1 = [features(1, i) for i in range(PACK)]
+            w1q1 = quantise_w1(raw1[a], "w1q1_%d" % a)
+            for i in range(PACK):
+                first_pass(banks1[i], a, w1q1, i, 0, S)
+        wg.append(scale_wgs(1, keep.tile([P, PACK, S], F32, name="wg1", tag="middle")))
+        for i in range(PACK):
+            gather(0, i, x0[:], 0, M)
+        th1 = [tanh(1, i, banks1[i], S) for i in range(PACK)]
+        x0_bf = round_x(x0[:], M)
+        scatter(1, 0, th1[0], 0, S)
+        tilt0_bf = make_tilt(0, x0[:], 0, M)
+        scatter(1, 1, th1[1], 0, S)
         xq0 = quantise(x0_bf, M, "xq0")
         tq0 = quantise(tilt0_bf, M, "tq0")
+        for i in range(2, PACK):
+            scatter(1, i, th1[i], 0, S)
         w3q = [quantise_w3(raw3[b], "w3q%d" % b) for b in range(H_PASSES)]
         for hf in range(2):
             second_product(0, hf, True, xq0, hf * HALF, None)
         for hf in range(2):
             second_product(0, hf, False, tq0, hf * HALF, w3q[0])
 
-        x1 = [keep.tile([P, PACK, HALF], F32, name="x1_%d" % hf) for hf in range(2)]
-        scatter(1, 0, h1[0])
+        x1_both = keep.tile([P, 2, PACK, HALF], F32, name="x1_both", tag="late")
+        x1 = [x1_both[:, hf, :, :] for hf in range(2)]
         for i in range(PACK):
-            if i + 1 < PACK:
-                scatter(1, i + 1, h1[i + 1])
             gather(1, i, x1[0], 0, HALF)
+        x_bf = [round_x(x1[0], HALF)]
+        gather(1, 0, x1[1], HALF, HALF)
+        tilt_bf = [make_tilt(1, x1[0], 0, HALF)]
+        for i in range(1, PACK):
+            gather(1, i, x1[1], HALF, HALF)
+        x_bf.append(round_x(x1[1], HALF))
         for hf in range(2):
-            if hf == 0:
-                x_bf = round_x(x1[0], HALF)
-                tilt_bf = make_tilt(1, x1[0], 0, HALF)
-                for i in range(PACK):
-                    gather(1, i, x1[1], HALF, HALF)
-            else:
-                x_bf = round_x(x1[1], HALF)
-                tilt_bf = make_tilt(1, x1[1], HALF, HALF)
-            xq = quantise(x_bf, HALF, "xq1_%d" % hf)
+            if hf == 1:
+                tilt_bf.append(make_tilt(1, x1[1], HALF, HALF))
+            xq = quantise(x_bf[hf], HALF, "xq1_%d" % hf)
             second_product(1, hf, True, xq, 0, None)
-            tq = quantise(tilt_bf, HALF, "tq1_%d" % hf)
+            tq = quantise(tilt_bf[hf], HALF, "tq1_%d" % hf)
             second_product(1, hf, False, tq, 0, w3q[1])
             for g in range(2):
                 store(hf, g, hf == 1 and g == 1)

@@ -32,9 +32,10 @@ def tile_list_tank_bay_gauging_kernel(
     nc = tc.nc
     with ExitStack() as ctx:
         keep = ctx.enter_context(tc.tile_pool(name="keep", bufs=1))
-        raw_pool = ctx.enter_context(tc.tile_pool(name="raw", bufs=5))
-        bf_pool = ctx.enter_context(tc.tile_pool(name="bf", bufs=5))
+        raw_pool = ctx.enter_context(tc.tile_pool(name="raw", bufs=4))
+        bf_pool = ctx.enter_context(tc.tile_pool(name="bf", bufs=6))
         h_pool = ctx.enter_context(tc.tile_pool(name="h", bufs=6))
+        late = ctx.enter_context(tc.tile_pool(name="late", bufs=1))
         psum = ctx.enter_context(tc.psum_pool(name="psum", bufs=1))
 
         idx = keep.tile([P, S // 16], U16, name="idx")
@@ -72,8 +73,9 @@ def tile_list_tank_bay_gauging_kernel(
         def load_att(b):
             nc.sync.dma_start(out=att_sb[b][:], in_=att[b * PASS:(b + 1) * PASS, :].rearrange("(p i) m -> p i m", i=PACK))
 
-        def quantise(grouped, width, name):
-            codes = keep.tile([P, width], U32, name=name + "_wd", align_bytes=64)
+        def quantise(grouped, width, name, codes=None):
+            if codes is None:
+                codes = keep.tile([P, width], U32, name=name + "_wd", align_bytes=64)
             scales = keep.tile([P, width], U8, name=name + "_sc", align_bytes=64)
             nc.vector.quantize_mx(out=codes[:].bitcast(FP8X4), scales=scales[:], in_=grouped)
             return codes, scales
@@ -161,6 +163,11 @@ def tile_list_tank_bay_gauging_kernel(
                 out=interleaved(grouped, width), in0=by_runs(x), in1=by_runs(att_sb[b][:, :, m0:m0 + width]), op=MULT
             )
             return grouped[:, 0:PACK * width]
+
+        def tilt_in_place(b, x, m0, width):
+            scores = att_sb[b][:, :, m0:m0 + width]
+            nc.vector.tensor_tensor(out=scores, in0=x, in1=scores, op=MULT)
+            return scores
 
         def second_product(b, hf, with_w2, moving, c0, w3q):
             codes, scales = moving
@@ -259,7 +266,7 @@ def tile_list_tank_bay_gauging_kernel(
         th0.append(tanh(0, 3, y_bank[0], S))
         raw3 = [load_rows(w3, 0, slice(0, N))]
         load_att(1)
-        raw3_last = keep.tile([P, PACK, PASS], F32, name="raw3_last", tag="late")
+        raw3_last = late.tile([P, PACK, PASS], F32, name="raw3_last", offset=0, align_bytes=64)
         nc.sync.dma_start(out=raw3_last[:], in_=w3[PASS:2 * PASS, :].rearrange("(p j) c -> p j c", j=PACK))
         raw3.append(raw3_last)
         x0 = keep.tile([P, PACK, M], F32, name="x0")
@@ -279,34 +286,34 @@ def tile_list_tank_bay_gauging_kernel(
         th1 = [tanh(1, i, banks1[i], S) for i in range(PACK)]
         x0_bf = round_x(x0[:], M)
         scatter(1, 0, th1[0], 0, S)
-        tilt0_bf = make_tilt(0, x0[:], 0, M)
+        tilt0_bf = round_x(tilt_in_place(0, x0[:], 0, M), M)
         scatter(1, 1, th1[1], 0, S)
         xq0 = quantise(x0_bf, M, "xq0")
-        tq0 = quantise(tilt0_bf, M, "tq0")
-        for i in range(2, PACK):
-            scatter(1, i, th1[i], 0, S)
+        scatter(1, 2, th1[2], 0, S)
+        scatter(1, 3, th1[3], 0, S)
         w3q = [quantise_w3(raw3[b], "w3q%d" % b) for b in range(H_PASSES)]
         for hf in range(2):
             second_product(0, hf, True, xq0, hf * HALF, None)
-        for hf in range(2):
-            second_product(0, hf, False, tq0, hf * HALF, w3q[0])
 
-        x1_both = keep.tile([P, 2, PACK, HALF], F32, name="x1_both", tag="late")
-        x1 = [x1_both[:, hf, :, :] for hf in range(2)]
+        x1 = [late.tile([P, PACK, HALF], F32, name="x1_%d" % hf, offset=hf * PACK * HALF * 4, align_bytes=64)[:] for hf in range(2)]
         for i in range(PACK):
             gather(1, i, x1[0], 0, HALF)
-        x_bf = [round_x(x1[0], HALF)]
+        x_bf = round_x(x1[0], HALF)
         gather(1, 0, x1[1], HALF, HALF)
-        tilt_bf = [make_tilt(1, x1[0], 0, HALF)]
-        for i in range(1, PACK):
-            gather(1, i, x1[1], HALF, HALF)
-        x_bf.append(round_x(x1[1], HALF))
+        tilt_bf = round_x(tilt_in_place(1, x1[0], 0, HALF), HALF)
+        gather(1, 1, x1[1], HALF, HALF)
+        second_product(1, 0, True, quantise(x_bf, HALF, "xq1_0"), 0, None)
+        tq0 = quantise(tilt0_bf, M, "tq0", late.tile([P, M], U32, name="tq0_wd", offset=0, align_bytes=64))
         for hf in range(2):
-            if hf == 1:
-                tilt_bf.append(make_tilt(1, x1[1], HALF, HALF))
-            xq = quantise(x_bf[hf], HALF, "xq1_%d" % hf)
-            second_product(1, hf, True, xq, 0, None)
-            tq = quantise(tilt_bf[hf], HALF, "tq1_%d" % hf)
-            second_product(1, hf, False, tq, 0, w3q[1])
-            for g in range(2):
-                store(hf, g, hf == 1 and g == 1)
+            second_product(0, hf, False, tq0, hf * HALF, w3q[0])
+        gather(1, 2, x1[1], HALF, HALF)
+        gather(1, 3, x1[1], HALF, HALF)
+        x_bf = round_x(x1[1], HALF)
+        second_product(1, 0, False, quantise(tilt_bf, HALF, "tq1_0"), 0, w3q[1])
+        tilt_bf = make_tilt(1, x1[1], HALF, HALF)
+        for g in range(2):
+            store(0, g, False)
+        second_product(1, 1, True, quantise(x_bf, HALF, "xq1_1"), 0, None)
+        second_product(1, 1, False, quantise(tilt_bf, HALF, "tq1_1"), 0, w3q[1])
+        for g in range(2):
+            store(1, g, g == 1)

@@ -201,13 +201,15 @@ def tile_list_tank_bay_gauging_kernel(
         half1 = slice(PASS, 2 * PASS)
 
         def load_table_scales(q):
-            nc.sync.dma_start(
+            nc.gpsimd.dma_start(
                 out=tab_sc[32 * q:32 * q + 4 * K_PASSES, :].bitcast(I32),
                 in_=tab_scales[:, 4 * q:4 * q + 4, :].bitcast(I32),
             )
 
         nc.gpsimd.memset(tab_sc[:].bitcast(I32), 0)
         make_identity(nc, ident[:])
+        for q in range(QUADS):
+            load_table_scales(q)
         nc.gpsimd.memset(w2_sc[:].bitcast(I32), 0)
         raw0 = [load_rows(w1, 0, half0)]
         nc.sync.dma_start(out=wgs_sb[:], in_=wgs)
@@ -215,8 +217,6 @@ def tile_list_tank_bay_gauging_kernel(
         nc.sync.dma_start(out=gn[:, :, 0:PACK], in_=gain.rearrange("(b p i) -> p b i", p=P, i=PACK))
         raw0.append(load_rows(w1, 2, half0))
         load_table(0)
-        for q in range(QUADS):
-            load_table_scales(q)
         nc.sync.dma_start(out=idx[:], in_=offs)
         load_table(1)
         load_table(2)

@@ -23,7 +23,12 @@ PASS = P * PACK
 K_PASSES = K // PASS
 H_PASSES = H // PASS
 QUADS = 4
-HALF = M // 2
+QUAD = P // QUADS
+GROUP = 16
+LINE = 4
+HALF_S = S // 2
+HALF_M = M // 2
+ALIGN = 64
 
 
 def tile_list_tank_bay_gauging_kernel(
@@ -38,31 +43,33 @@ def tile_list_tank_bay_gauging_kernel(
         late = ctx.enter_context(tc.tile_pool(name="late", bufs=1))
         psum = ctx.enter_context(tc.psum_pool(name="psum", bufs=1))
 
-        idx = keep.tile([P, S // 16], U16, name="idx")
-        idx2 = keep.tile([P, S // 16], U16, name="idx2")
-        idx3 = keep.tile([P, M // 16], U16, name="idx3")
-        tab_sc = keep.tile([P, T], U8, name="tab_sc", align_bytes=64)
-        w2_sc = keep.tile([P, H_PASSES, N], U8, name="w2_sc", align_bytes=64)
-        w2_wd = keep.tile([P, H_PASSES, 2 * N], U8, name="w2_wd", align_bytes=64)
+        idx = keep.tile([P, S // GROUP], U16, name="idx")
+        idx2 = keep.tile([P, S // GROUP], U16, name="idx2")
+        idx3 = keep.tile([P, M // GROUP], U16, name="idx3")
+        tab_sc = keep.tile([P, T], U8, name="tab_sc", align_bytes=ALIGN)
+        w2_sc = keep.tile([P, H_PASSES, N], U8, name="w2_sc", align_bytes=ALIGN)
+        w2_wd = keep.tile([P, H_PASSES, 2 * N], U8, name="w2_wd", align_bytes=ALIGN)
         bias = keep.tile([P, H_PASSES, 2 * PACK], F32, name="bias")
         gn = keep.tile([P, H_PASSES, 2 * PACK], F32, name="gn")
         wgs_sb = keep.tile([P, S], F32, name="wgs_sb")
         ident = keep.tile([P, P], F32, name="ident")
         wgt_sb = keep.tile([P, M], F32, name="wgt_sb")
-        tab_wd = [keep.tile([P, T], I32, name="tab_wd%d" % a, align_bytes=64) for a in range(K_PASSES)]
-        v_wd = [keep.tile([P, S], U32, name="v_wd%d" % a, align_bytes=64) for a in range(K_PASSES)]
-        v_sc = keep.tile([P, S], U8, name="v_sc", align_bytes=64)
+        tab_wd = [keep.tile([P, T], I32, name="tab_wd%d" % a, align_bytes=ALIGN) for a in range(K_PASSES)]
+        v_wd = [keep.tile([P, S], U32, name="v_wd%d" % a, align_bytes=ALIGN) for a in range(K_PASSES)]
+        v_sc = keep.tile([P, S], U8, name="v_sc", align_bytes=ALIGN)
         page = [[keep.tile([P, T2], F32, name="page%d_%d" % (b, i)) for i in range(PACK)] for b in range(H_PASSES)]
         att_sb = [keep.tile([P, PACK, M], F32, name="att%d" % b) for b in range(H_PASSES)]
         y_bank = [psum.tile([P, S], F32, name="y%d" % i) for i in range(PACK)]
-        out_bank = [[psum.tile([P, 2, HALF], F32, name="o%d_%d" % (hf, g)) for g in range(2)] for hf in range(2)]
+        out_bank = [[psum.tile([P, 2, HALF_M], F32, name="o%d_%d" % (hf, g)) for g in range(2)] for hf in range(2)]
 
         page_rows = page0.rearrange("(b p i) t -> b i p t", p=P, i=PACK)
 
-        def load_rows(w, a, cols):
-            raw = raw_pool.tile([P, PACK, PASS], F32, name="raw", tag="raw")
+        def load_pass(raw, w, a, cols):
             nc.sync.dma_start(out=raw[:], in_=w[a * PASS:(a + 1) * PASS, cols].rearrange("(p j) c -> p j c", j=PACK))
             return raw
+
+        def load_staged(w, a, cols):
+            return load_pass(raw_pool.tile([P, PACK, PASS], F32, name="raw", tag="raw"), w, a, cols)
 
         def load_table(a):
             nc.sync.dma_start(out=tab_wd[a][:], in_=tab_words[a].rearrange("p t i -> p (t i)").bitcast(I32))
@@ -70,38 +77,42 @@ def tile_list_tank_bay_gauging_kernel(
         def load_page(b, i):
             nc.sync.dma_start(out=page[b][i][:], in_=page_rows[b, i])
 
-        def load_att(b):
-            nc.sync.dma_start(out=att_sb[b][:], in_=att[b * PASS:(b + 1) * PASS, :].rearrange("(p i) m -> p i m", i=PACK))
+        def new_codes(width, name):
+            return keep.tile([P, width], U32, name=name + "_wd", align_bytes=ALIGN)
 
-        def quantise(grouped, width, name, codes=None):
-            if codes is None:
-                codes = keep.tile([P, width], U32, name=name + "_wd", align_bytes=64)
-            scales = keep.tile([P, width], U8, name=name + "_sc", align_bytes=64)
+        def quantise(grouped, codes, name):
+            scales = keep.tile([P, codes.shape[1]], U8, name=name + "_sc", align_bytes=ALIGN)
             nc.vector.quantize_mx(out=codes[:].bitcast(FP8X4), scales=scales[:], in_=grouped)
             return codes, scales
 
-        def quantise_w1(raw, name):
-            grouped = bf_pool.tile([P, PACK * PASS], BF16, name="grouped", align_bytes=64)
-            nc.scalar.copy(
+        def quantise_new(grouped, width, name):
+            return quantise(grouped, new_codes(width, name), name)
+
+        def quantise_w1(raw, name, copy):
+            grouped = bf_pool.tile([P, PACK * PASS], BF16, name="grouped", align_bytes=ALIGN)
+            copy(
                 out=grouped[:].rearrange("p (t m j) -> p m j t", t=PACK, j=PACK),
                 in_=raw[:].rearrange("p j (m t) -> p m j t", t=PACK),
             )
-            return quantise(grouped[:], PASS, name)
+            return quantise_new(grouped[:], PASS, name)
 
         def interleaved(tile, width):
-            return tile[:, 0:PACK * width].rearrange("p (c i t) -> p c t i", i=4, t=PACK)
+            return tile[:, 0:PACK * width].rearrange("p (c i t) -> p c t i", i=LINE, t=PACK)
 
-        def by_runs(ap):
-            return ap.rearrange("p t (c i) -> p c t i", i=4)
+        def by_lines(rows):
+            return rows.rearrange("p t (c i) -> p c t i", i=LINE)
 
-        def quantise_w3(raw, name):
-            grouped = bf_pool.tile([P, PACK * PASS], BF16, name="grouped", align_bytes=64)
-            nc.scalar.copy(out=interleaved(grouped, N), in_=by_runs(raw[:]))
-            return quantise(grouped[:], N, name)
+        def round_rows(rows, width):
+            grouped = bf_pool.tile([P, PACK * PASS], BF16, name="grouped", align_bytes=ALIGN)
+            nc.scalar.copy(out=interleaved(grouped, width), in_=by_lines(rows))
+            return grouped[:, 0:PACK * width]
+
+        def entries(offsets, first, count):
+            return offsets[:, first // GROUP:(first + count) // GROUP]
 
         def gather_table(a, j0, width):
             nc.vector.tensor_copy(
-                out=v_wd[a][:, j0:j0 + width], in_=tab_wd[a][:].bitcast(U32).indirect(idx[:, j0 // 16:(j0 + width) // 16])
+                out=v_wd[a][:, j0:j0 + width], in_=tab_wd[a][:].bitcast(U32).indirect(entries(idx, j0, width))
             )
 
         def first_pass(bank, a, w1q, i, j0, width):
@@ -119,16 +130,11 @@ def tile_list_tank_bay_gauging_kernel(
             nc.scalar.activation(out=th[:, 0:width], in_=bank[:, 0:width], func=ACT.Tanh, bias=bias[:, b, i:i + 1])
             return th[:, 0:width]
 
-        def scatter(b, i, th, j0, width):
+        def scatter(b, i, th, factors, j0, width):
             nc.vector.tensor_tensor(
-                out=page[b][i][:].indirect(idx2[:, j0 // 16:(j0 + width) // 16]),
-                in0=th, in1=wg[b][:, i, j0:j0 + width], op=MULT,
+                out=page[b][i][:].indirect(entries(idx2, j0, width)),
+                in0=th, in1=factors[:, i, j0:j0 + width], op=MULT,
             )
-
-        def scale_wgs(b, scaled):
-            for i in range(PACK):
-                nc.scalar.activation(out=scaled[:, i, :], in_=wgs_bank(i), func=ACT.Copy, scale=gn[:, b, i:i + 1])
-            return scaled
 
         def wgs_bank(i):
             return out_bank[i // 2][i % 2][:].rearrange("p u m -> p (u m)")
@@ -148,74 +154,75 @@ def tile_list_tank_bay_gauging_kernel(
                         out=wgs_bank(i)[:, jb * P:(jb + 1) * P], in_=dealt[:, jb, i * P:(i + 1) * P], identity=ident[:]
                     )
 
+        def scatter_factors(b, factors):
+            for i in range(PACK):
+                nc.scalar.activation(out=factors[:, i, :], in_=wgs_bank(i), func=ACT.Copy, scale=gn[:, b, i:i + 1])
+            return factors
+
         def gather(b, i, x, m0, width):
-            offsets = idx3[:, m0 // 16:(m0 + width) // 16]
-            nc.vector.tensor_tensor(out=x[:, i, :], in0=page[b][i][:].indirect(offsets), in1=wgt_sb[:, m0:m0 + width], op=MULT)
-
-        def round_x(x, width):
-            grouped = bf_pool.tile([P, PACK * PASS], BF16, name="grouped", align_bytes=64)
-            nc.scalar.copy(out=interleaved(grouped, width), in_=by_runs(x))
-            return grouped[:, 0:PACK * width]
-
-        def make_tilt(b, x, m0, width):
-            grouped = bf_pool.tile([P, PACK * PASS], BF16, name="grouped", align_bytes=64)
             nc.vector.tensor_tensor(
-                out=interleaved(grouped, width), in0=by_runs(x), in1=by_runs(att_sb[b][:, :, m0:m0 + width]), op=MULT
+                out=x[:, i, :], in0=page[b][i][:].indirect(entries(idx3, m0, width)), in1=wgt_sb[:, m0:m0 + width], op=MULT
             )
-            return grouped[:, 0:PACK * width]
 
         def tilt_in_place(b, x, m0, width):
             scores = att_sb[b][:, :, m0:m0 + width]
             nc.vector.tensor_tensor(out=scores, in0=x, in1=scores, op=MULT)
             return scores
 
-        def second_product(b, hf, with_w2, moving, c0, w3q):
+        def tilt_rounded(b, x, m0, width):
+            grouped = bf_pool.tile([P, PACK * PASS], BF16, name="grouped", align_bytes=ALIGN)
+            nc.vector.tensor_tensor(
+                out=interleaved(grouped, width), in0=by_lines(x), in1=by_lines(att_sb[b][:, :, m0:m0 + width]), op=MULT
+            )
+            return grouped[:, 0:PACK * width]
+
+        def second_passes(hf, stationary, moving, c0, opens, closes):
             codes, scales = moving
-            cols = slice(c0, c0 + HALF)
+            cols = slice(c0, c0 + HALF_M)
             for nt in range(N // P):
-                n_cols = slice(nt * P, (nt + 1) * P)
-                if with_w2:
-                    lhsT = w2_wd[:, b, 2 * nt * P:2 * (nt + 1) * P].bitcast(FP4X4)
-                    lhsT_scale = w2_sc[:, b, n_cols]
-                else:
-                    lhsT = w3q[0][:, n_cols].bitcast(FP8X4)
-                    lhsT_scale = w3q[1][:, n_cols]
+                lhsT, lhsT_scale = stationary(nt)
                 nc.tensor.matmul_mx(
                     out=out_bank[hf][nt // 2][:, nt % 2, :],
                     lhsT=lhsT, lhsT_scale=lhsT_scale,
                     rhs=codes[:, cols].bitcast(FP8X4), rhs_scale=scales[:, cols],
-                    start=(b == 0 and with_w2 and nt % 2 == 0),
-                    stop=(b == H_PASSES - 1 and not with_w2 and nt % 2 == 1),
+                    start=(opens and nt % 2 == 0), stop=(closes and nt % 2 == 1),
                 )
 
-        def store(hf, g, on_vector):
-            res = keep.tile([P, 2, HALF], F32, name="res%d_%d" % (hf, g))
-            if on_vector:
-                nc.vector.tensor_copy(out=res[:], in_=out_bank[hf][g][:])
-            else:
-                nc.scalar.copy(out=res[:], in_=out_bank[hf][g][:])
-            rows = out[2 * g * P:2 * (g + 1) * P, hf * HALF:(hf + 1) * HALF]
+        def x_passes(b, hf, xq, c0):
+            second_passes(
+                hf, lambda nt: (w2_wd[:, b, 2 * nt * P:2 * (nt + 1) * P].bitcast(FP4X4), w2_sc[:, b, nt * P:(nt + 1) * P]),
+                xq, c0, b == 0, False,
+            )
+
+        def tilt_passes(b, hf, tq, c0, w3q):
+            codes, scales = w3q
+            second_passes(
+                hf, lambda nt: (codes[:, nt * P:(nt + 1) * P].bitcast(FP8X4), scales[:, nt * P:(nt + 1) * P]),
+                tq, c0, False, b == H_PASSES - 1,
+            )
+
+        def store(hf, g, copy):
+            res = keep.tile([P, 2, HALF_M], F32, name="res%d_%d" % (hf, g))
+            copy(out=res[:], in_=out_bank[hf][g][:])
+            rows = out[2 * g * P:2 * (g + 1) * P, hf * HALF_M:(hf + 1) * HALF_M]
             nc.sync.dma_start(out=rows.rearrange("(u p) m -> p u m", p=P), in_=res[:])
 
-        half0 = slice(0, PASS)
-        half1 = slice(PASS, 2 * PASS)
-
-        def load_table_scales(q):
-            nc.gpsimd.dma_start(
-                out=tab_sc[32 * q:32 * q + 4 * K_PASSES, :].bitcast(I32),
-                in_=tab_scales[:, 4 * q:4 * q + 4, :].bitcast(I32),
-            )
+        r_cols = [slice(b * PASS, (b + 1) * PASS) for b in range(H_PASSES)]
+        last = K_PASSES - 1
 
         nc.gpsimd.memset(tab_sc[:].bitcast(I32), 0)
         make_identity(nc, ident[:])
         for q in range(QUADS):
-            load_table_scales(q)
+            nc.gpsimd.dma_start(
+                out=tab_sc[QUAD * q:QUAD * q + 4 * K_PASSES, :].bitcast(I32),
+                in_=tab_scales[:, 4 * q:4 * q + 4, :].bitcast(I32),
+            )
         nc.gpsimd.memset(w2_sc[:].bitcast(I32), 0)
-        raw0 = [load_rows(w1, 0, half0)]
+        raw0 = [load_staged(w1, 0, r_cols[0])]
         nc.sync.dma_start(out=wgs_sb[:], in_=wgs)
-        raw0.append(load_rows(w1, 1, half0))
+        raw0.append(load_staged(w1, 1, r_cols[0]))
         nc.sync.dma_start(out=gn[:, :, 0:PACK], in_=gain.rearrange("(b p i) -> p b i", p=P, i=PACK))
-        raw0.append(load_rows(w1, 2, half0))
+        raw0.append(load_staged(w1, 2, r_cols[0]))
         load_table(0)
         nc.sync.dma_start(out=idx[:], in_=offs)
         load_table(1)
@@ -226,94 +233,94 @@ def tile_list_tank_bay_gauging_kernel(
             load_page(0, i)
         nc.sync.dma_start(out=idx3[:], in_=offs3)
         deal_wgs()
-        raw1 = [load_rows(w1, a, half1) for a in range(K_PASSES - 1)]
-        raw1_last = keep.tile([P, PACK, PASS], F32, name="raw1_last", tag="middle")
-        nc.sync.dma_start(out=raw1_last[:], in_=w1[(K_PASSES - 1) * PASS:K, half1].rearrange("(p j) c -> p j c", j=PACK))
-        raw1.append(raw1_last)
+        raw1 = [load_staged(w1, a, r_cols[1]) for a in range(last)]
+        raw1.append(load_pass(keep.tile([P, PACK, PASS], F32, name="raw1_last", tag="middle"), w1, last, r_cols[1]))
         nc.sync.dma_start(out=wgt_sb[:], in_=wgt)
         load_page(1, 0)
-        load_att(0)
+        load_pass(att_sb[0], att, 0, slice(0, M))
         for i in range(1, PACK):
             load_page(1, i)
         nc.sync.dma_start(out=w2_wd[:].bitcast(I32), in_=w2_words.rearrange("a p c -> p a c").bitcast(I32))
         for q in range(QUADS):
             nc.sync.dma_start(
-                out=w2_sc[32 * q:32 * q + 4, :, :].bitcast(I32),
+                out=w2_sc[QUAD * q:QUAD * q + 4, :, :].bitcast(I32),
                 in_=w2_scales[:, 4 * q:4 * q + 4, :].rearrange("a r n -> r a n").bitcast(I32),
             )
 
         nc.vector.tensor_copy(out=v_sc[:], in_=tab_sc[:].indirect(idx[:]))
-        w1q = [quantise_w1(raw0[a], "w1q0_%d" % a) for a in range(K_PASSES)]
-        wg = [scale_wgs(0, keep.tile([P, PACK, S], F32, name="wg0"))]
-        last = K_PASSES - 1
+        casts = [nc.scalar.copy] * last + [nc.vector.tensor_copy]
+        w1q = [quantise_w1(raw0[a], "w1q0_%d" % a, casts[a]) for a in range(K_PASSES)]
+        factors0 = scatter_factors(0, keep.tile([P, PACK, S], F32, name="wg0"))
         for a in range(last):
             gather_table(a, 0, S)
             for hs in range(2):
-                first_pass(y_bank[hs], a, w1q[a], 0, hs * S // 2, S // 2)
+                first_pass(y_bank[hs], a, w1q[a], 0, hs * HALF_S, HALF_S)
             for i in (1, 2):
                 first_pass(y_bank[i + 1], a, w1q[a], i, 0, S)
-        th00 = []
+        th_halves = []
         for hs in range(2):
-            gather_table(last, hs * S // 2, S // 2)
-            first_pass(y_bank[hs], last, w1q[last], 0, hs * S // 2, S // 2)
-            th00.append(tanh(0, 0, y_bank[hs], S // 2))
-        th0 = [None]
+            gather_table(last, hs * HALF_S, HALF_S)
+            first_pass(y_bank[hs], last, w1q[last], 0, hs * HALF_S, HALF_S)
+            th_halves.append(tanh(0, 0, y_bank[hs], HALF_S))
+        th0 = {}
         for i in (1, 2):
             first_pass(y_bank[i + 1], last, w1q[last], i, 0, S)
-            th0.append(tanh(0, i, y_bank[i + 1], S))
+            th0[i] = tanh(0, i, y_bank[i + 1], S)
         for a in range(K_PASSES):
             first_pass(y_bank[0], a, w1q[a], 3, 0, S)
-        th0.append(tanh(0, 3, y_bank[0], S))
-        raw3 = [load_rows(w3, 0, slice(0, N))]
-        load_att(1)
-        raw3_last = late.tile([P, PACK, PASS], F32, name="raw3_last", offset=0, align_bytes=64)
-        nc.sync.dma_start(out=raw3_last[:], in_=w3[PASS:2 * PASS, :].rearrange("(p j) c -> p j c", j=PACK))
-        raw3.append(raw3_last)
+        th0[3] = tanh(0, 3, y_bank[0], S)
+        raw3 = [load_staged(w3, 0, slice(0, N))]
+        load_pass(att_sb[1], att, 1, slice(0, M))
+        raw3.append(load_pass(late.tile([P, PACK, PASS], F32, name="raw3_last", offset=0, align_bytes=ALIGN), w3, 1, slice(0, N)))
         x0 = keep.tile([P, PACK, M], F32, name="x0")
         for hs in range(2):
-            scatter(0, 0, th00[hs], hs * S // 2, S // 2)
+            scatter(0, 0, th_halves[hs], factors0, hs * HALF_S, HALF_S)
         for i in range(1, PACK):
-            scatter(0, i, th0[i], 0, S)
+            scatter(0, i, th0[i], factors0, 0, S)
 
         banks1 = [y_bank[(i + 1) % PACK] for i in range(PACK)]
         for a in range(K_PASSES):
-            w1q1 = quantise_w1(raw1[a], "w1q1_%d" % a)
+            w1q1 = quantise_w1(raw1[a], "w1q1_%d" % a, nc.scalar.copy)
             for i in range(PACK):
                 first_pass(banks1[i], a, w1q1, i, 0, S)
-        wg.append(scale_wgs(1, keep.tile([P, PACK, S], F32, name="wg1", tag="middle")))
+        factors1 = scatter_factors(1, keep.tile([P, PACK, S], F32, name="wg1", tag="middle"))
         for i in range(PACK):
             gather(0, i, x0[:], 0, M)
         th1 = [tanh(1, i, banks1[i], S) for i in range(PACK)]
-        x0_bf = round_x(x0[:], M)
-        scatter(1, 0, th1[0], 0, S)
-        tilt0_bf = round_x(tilt_in_place(0, x0[:], 0, M), M)
-        scatter(1, 1, th1[1], 0, S)
-        xq0 = quantise(x0_bf, M, "xq0")
-        scatter(1, 2, th1[2], 0, S)
-        scatter(1, 3, th1[3], 0, S)
-        w3q = [quantise_w3(raw3[b], "w3q%d" % b) for b in range(H_PASSES)]
+        x0_bf = round_rows(x0[:], M)
+        scatter(1, 0, th1[0], factors1, 0, S)
+        tilt0_bf = round_rows(tilt_in_place(0, x0[:], 0, M), M)
+        scatter(1, 1, th1[1], factors1, 0, S)
+        xq0 = quantise_new(x0_bf, M, "xq0")
+        scatter(1, 2, th1[2], factors1, 0, S)
+        scatter(1, 3, th1[3], factors1, 0, S)
+        w3q = [quantise_new(round_rows(raw3[b][:], N), N, "w3q%d" % b) for b in range(H_PASSES)]
         for hf in range(2):
-            second_product(0, hf, True, xq0, hf * HALF, None)
+            x_passes(0, hf, xq0, hf * HALF_M)
 
-        x1 = [late.tile([P, PACK, HALF], F32, name="x1_%d" % hf, offset=hf * PACK * HALF * 4, align_bytes=64)[:] for hf in range(2)]
+        half_bytes = PACK * HALF_M * 4
+        x1 = [
+            late.tile([P, PACK, HALF_M], F32, name="x1_%d" % hf, offset=hf * half_bytes, align_bytes=ALIGN)[:]
+            for hf in range(2)
+        ]
         for i in range(PACK):
-            gather(1, i, x1[0], 0, HALF)
-        x_bf = round_x(x1[0], HALF)
-        gather(1, 0, x1[1], HALF, HALF)
-        tilt_bf = round_x(tilt_in_place(1, x1[0], 0, HALF), HALF)
-        gather(1, 1, x1[1], HALF, HALF)
-        second_product(1, 0, True, quantise(x_bf, HALF, "xq1_0"), 0, None)
-        tq0 = quantise(tilt0_bf, M, "tq0", late.tile([P, M], U32, name="tq0_wd", offset=0, align_bytes=64))
+            gather(1, i, x1[0], 0, HALF_M)
+        x1_bf0 = round_rows(x1[0], HALF_M)
+        gather(1, 0, x1[1], HALF_M, HALF_M)
+        tilt1_bf0 = round_rows(tilt_in_place(1, x1[0], 0, HALF_M), HALF_M)
+        gather(1, 1, x1[1], HALF_M, HALF_M)
+        x_passes(1, 0, quantise_new(x1_bf0, HALF_M, "xq1_0"), 0)
+        tq0 = quantise(tilt0_bf, late.tile([P, M], U32, name="tq0_wd", offset=0, align_bytes=ALIGN), "tq0")
         for hf in range(2):
-            second_product(0, hf, False, tq0, hf * HALF, w3q[0])
-        gather(1, 2, x1[1], HALF, HALF)
-        gather(1, 3, x1[1], HALF, HALF)
-        x_bf = round_x(x1[1], HALF)
-        second_product(1, 0, False, quantise(tilt_bf, HALF, "tq1_0"), 0, w3q[1])
-        tilt_bf = make_tilt(1, x1[1], HALF, HALF)
+            tilt_passes(0, hf, tq0, hf * HALF_M, w3q[0])
+        gather(1, 2, x1[1], HALF_M, HALF_M)
+        gather(1, 3, x1[1], HALF_M, HALF_M)
+        x1_bf1 = round_rows(x1[1], HALF_M)
+        tilt_passes(1, 0, quantise_new(tilt1_bf0, HALF_M, "tq1_0"), 0, w3q[1])
+        tilt1_bf1 = tilt_rounded(1, x1[1], HALF_M, HALF_M)
         for g in range(2):
-            store(0, g, False)
-        second_product(1, 1, True, quantise(x_bf, HALF, "xq1_1"), 0, None)
-        second_product(1, 1, False, quantise(tilt_bf, HALF, "tq1_1"), 0, w3q[1])
-        for g in range(2):
-            store(1, g, g == 1)
+            store(0, g, nc.scalar.copy)
+        x_passes(1, 1, quantise_new(x1_bf1, HALF_M, "xq1_1"), 0)
+        tilt_passes(1, 1, quantise_new(tilt1_bf1, HALF_M, "tq1_1"), 0, w3q[1])
+        store(1, 0, nc.scalar.copy)
+        store(1, 1, nc.vector.tensor_copy)

from contextlib import ExitStack

import concourse.mybir as mybir
from concourse.masks import make_identity

K, T, S, H, T2, M, N = 1536, 2048, 512, 1024, 1024, 512, 512
FLOPS = 2 * K * H * S + 2 * 2 * H * N * M

F32 = mybir.dt.float32
BF16 = mybir.dt.bfloat16
I32 = mybir.dt.int32
U32 = mybir.dt.uint32
U16 = mybir.dt.uint16
U8 = mybir.dt.uint8
FP8X4 = mybir.dt.float8_e4m3fn_x4
FP4X4 = mybir.dt.float4_e2m1fn_x4
MULT = mybir.AluOpType.mult
ACT = mybir.ActivationFunctionType

P = 128
PACK = 4
PASS = P * PACK
K_PASSES = K // PASS
H_PASSES = H // PASS
QUADS = 4
QUAD = P // QUADS
GROUP = 16
LINE = 4
HALF_S = S // 2
HALF_M = M // 2
ALIGN = 64


def tile_list_tank_bay_gauging_kernel(
    tc, tab_words, tab_scales, offs, offs2, offs3, w1, b1, gain, wgs, page0, wgt, att, w2_words, w2_scales, w3, out
):
    nc = tc.nc
    with ExitStack() as ctx:
        keep = ctx.enter_context(tc.tile_pool(name="keep", bufs=1))
        raw_pool = ctx.enter_context(tc.tile_pool(name="raw", bufs=4))
        bf_pool = ctx.enter_context(tc.tile_pool(name="bf", bufs=6))
        h_pool = ctx.enter_context(tc.tile_pool(name="h", bufs=6))
        late = ctx.enter_context(tc.tile_pool(name="late", bufs=1))
        psum = ctx.enter_context(tc.psum_pool(name="psum", bufs=1))

        idx = keep.tile([P, S // GROUP], U16, name="idx")
        idx2 = keep.tile([P, S // GROUP], U16, name="idx2")
        idx3 = keep.tile([P, M // GROUP], U16, name="idx3")
        tab_sc = keep.tile([P, T], U8, name="tab_sc", align_bytes=ALIGN)
        w2_sc = keep.tile([P, H_PASSES, N], U8, name="w2_sc", align_bytes=ALIGN)
        w2_wd = keep.tile([P, H_PASSES, 2 * N], U8, name="w2_wd", align_bytes=ALIGN)
        bias = keep.tile([P, H_PASSES, 2 * PACK], F32, name="bias")
        gn = keep.tile([P, H_PASSES, 2 * PACK], F32, name="gn")
        wgs_sb = keep.tile([P, S], F32, name="wgs_sb")
        ident = keep.tile([P, P], F32, name="ident")
        wgt_sb = keep.tile([P, M], F32, name="wgt_sb")
        tab_wd = [keep.tile([P, T], I32, name="tab_wd%d" % a, align_bytes=ALIGN) for a in range(K_PASSES)]
        v_wd = [keep.tile([P, S], U32, name="v_wd%d" % a, align_bytes=ALIGN) for a in range(K_PASSES)]
        v_sc = keep.tile([P, S], U8, name="v_sc", align_bytes=ALIGN)
        page = [[keep.tile([P, T2], F32, name="page%d_%d" % (b, i)) for i in range(PACK)] for b in range(H_PASSES)]
        att_sb = [keep.tile([P, PACK, M], F32, name="att%d" % b) for b in range(H_PASSES)]
        y_bank = [psum.tile([P, S], F32, name="y%d" % i) for i in range(PACK)]
        out_bank = [[psum.tile([P, 2, HALF_M], F32, name="o%d_%d" % (hf, g)) for g in range(2)] for hf in range(2)]

        page_rows = page0.rearrange("(b p i) t -> b i p t", p=P, i=PACK)

        def load_pass(raw, w, a, cols):
            nc.sync.dma_start(out=raw[:], in_=w[a * PASS:(a + 1) * PASS, cols].rearrange("(p j) c -> p j c", j=PACK))
            return raw

        def load_staged(w, a, cols):
            return load_pass(raw_pool.tile([P, PACK, PASS], F32, name="raw", tag="raw"), w, a, cols)

        def load_table(a):
            nc.sync.dma_start(out=tab_wd[a][:], in_=tab_words[a].rearrange("p t i -> p (t i)").bitcast(I32))

        def load_page(b, i):
            nc.sync.dma_start(out=page[b][i][:], in_=page_rows[b, i])

        def new_codes(width, name):
            return keep.tile([P, width], U32, name=name + "_wd", align_bytes=ALIGN)

        def quantise(grouped, codes, name):
            scales = keep.tile([P, codes.shape[1]], U8, name=name + "_sc", align_bytes=ALIGN)
            nc.vector.quantize_mx(out=codes[:].bitcast(FP8X4), scales=scales[:], in_=grouped)
            return codes, scales

        def quantise_new(grouped, width, name):
            return quantise(grouped, new_codes(width, name), name)

        def quantise_w1(raw, name, copy):
            grouped = bf_pool.tile([P, PACK * PASS], BF16, name="grouped", align_bytes=ALIGN)
            copy(
                out=grouped[:].rearrange("p (t m j) -> p m j t", t=PACK, j=PACK),
                in_=raw[:].rearrange("p j (m t) -> p m j t", t=PACK),
            )
            return quantise_new(grouped[:], PASS, name)

        def interleaved(tile, width):
            return tile[:, 0:PACK * width].rearrange("p (c i t) -> p c t i", i=LINE, t=PACK)

        def by_lines(rows):
            return rows.rearrange("p t (c i) -> p c t i", i=LINE)

        def round_rows(rows, width):
            grouped = bf_pool.tile([P, PACK * PASS], BF16, name="grouped", align_bytes=ALIGN)
            nc.scalar.copy(out=interleaved(grouped, width), in_=by_lines(rows))
            return grouped[:, 0:PACK * width]

        def entries(offsets, first, count):
            return offsets[:, first // GROUP:(first + count) // GROUP]

        def gather_table(a, j0, width):
            nc.vector.tensor_copy(
                out=v_wd[a][:, j0:j0 + width], in_=tab_wd[a][:].bitcast(U32).indirect(entries(idx, j0, width))
            )

        def first_pass(bank, a, w1q, i, j0, width):
            codes, scales = w1q
            cols = slice(i * P, (i + 1) * P)
            nc.tensor.matmul_mx(
                out=bank[:, 0:width],
                lhsT=codes[:, cols].bitcast(FP8X4), lhsT_scale=scales[:, cols],
                rhs=v_wd[a][:, j0:j0 + width].bitcast(FP8X4), rhs_scale=v_sc[4 * a:P, j0:j0 + width],
                start=(a == 0), stop=(a == K_PASSES - 1),
            )

        def tanh(b, i, bank, width):
            th = h_pool.tile([P, S], F32, name="th")
            nc.scalar.activation(out=th[:, 0:width], in_=bank[:, 0:width], func=ACT.Tanh, bias=bias[:, b, i:i + 1])
            return th[:, 0:width]

        def scatter(b, i, th, factors, j0, width):
            nc.vector.tensor_tensor(
                out=page[b][i][:].indirect(entries(idx2, j0, width)),
                in0=th, in1=factors[:, i, j0:j0 + width], op=MULT,
            )

        def wgs_bank(i):
            return out_bank[i // 2][i % 2][:].rearrange("p u m -> p (u m)")

        def deal_wgs():
            turned = y_bank[PACK - 1]
            for jb in range(S // P):
                nc.tensor.transpose(out=turned[:, jb * P:(jb + 1) * P], in_=wgs_sb[:, jb * P:(jb + 1) * P], identity=ident[:])
            dealt = raw_pool.tile([P, PACK, PASS], F32, name="dealt", tag="raw")
            parts = dealt[:].rearrange("p jb (i r q) -> p jb i r q", i=PACK, r=QUADS)
            nc.vector.tensor_copy(out=parts[:, :, :, 0, :], in_=turned[:].rearrange("p (jb q i) -> p jb i q", jb=S // P, i=PACK))
            nc.vector.tensor_copy(out=parts[:, :, :, 1, :], in_=parts[:, :, :, 0, :])
            nc.vector.tensor_copy(out=parts[:, :, :, 2:4, :], in_=parts[:, :, :, 0:2, :])
            for i in range(PACK):
                for jb in range(S // P):
                    nc.tensor.transpose(
                        out=wgs_bank(i)[:, jb * P:(jb + 1) * P], in_=dealt[:, jb, i * P:(i + 1) * P], identity=ident[:]
                    )

        def scatter_factors(b, factors):
            for i in range(PACK):
                nc.scalar.activation(out=factors[:, i, :], in_=wgs_bank(i), func=ACT.Copy, scale=gn[:, b, i:i + 1])
            return factors

        def gather(b, i, x, m0, width):
            nc.vector.tensor_tensor(
                out=x[:, i, :], in0=page[b][i][:].indirect(entries(idx3, m0, width)), in1=wgt_sb[:, m0:m0 + width], op=MULT
            )

        def tilt_in_place(b, x, m0, width):
            scores = att_sb[b][:, :, m0:m0 + width]
            nc.vector.tensor_tensor(out=scores, in0=x, in1=scores, op=MULT)
            return scores

        def tilt_rounded(b, x, m0, width):
            grouped = bf_pool.tile([P, PACK * PASS], BF16, name="grouped", align_bytes=ALIGN)
            nc.vector.tensor_tensor(
                out=interleaved(grouped, width), in0=by_lines(x), in1=by_lines(att_sb[b][:, :, m0:m0 + width]), op=MULT
            )
            return grouped[:, 0:PACK * width]

        def second_passes(hf, stationary, moving, c0, opens, closes):
            codes, scales = moving
            cols = slice(c0, c0 + HALF_M)
            for nt in range(N // P):
                lhsT, lhsT_scale = stationary(nt)
                nc.tensor.matmul_mx(
                    out=out_bank[hf][nt // 2][:, nt % 2, :],
                    lhsT=lhsT, lhsT_scale=lhsT_scale,
                    rhs=codes[:, cols].bitcast(FP8X4), rhs_scale=scales[:, cols],
                    start=(opens and nt % 2 == 0), stop=(closes and nt % 2 == 1),
                )

        def x_passes(b, hf, xq, c0):
            second_passes(
                hf, lambda nt: (w2_wd[:, b, 2 * nt * P:2 * (nt + 1) * P].bitcast(FP4X4), w2_sc[:, b, nt * P:(nt + 1) * P]),
                xq, c0, b == 0, False,
            )

        def tilt_passes(b, hf, tq, c0, w3q):
            codes, scales = w3q
            second_passes(
                hf, lambda nt: (codes[:, nt * P:(nt + 1) * P].bitcast(FP8X4), scales[:, nt * P:(nt + 1) * P]),
                tq, c0, False, b == H_PASSES - 1,
            )

        def store(hf, g, copy):
            res = keep.tile([P, 2, HALF_M], F32, name="res%d_%d" % (hf, g))
            copy(out=res[:], in_=out_bank[hf][g][:])
            rows = out[2 * g * P:2 * (g + 1) * P, hf * HALF_M:(hf + 1) * HALF_M]
            nc.sync.dma_start(out=rows.rearrange("(u p) m -> p u m", p=P), in_=res[:])

        r_cols = [slice(b * PASS, (b + 1) * PASS) for b in range(H_PASSES)]
        last = K_PASSES - 1

        nc.gpsimd.memset(tab_sc[:].bitcast(I32), 0)
        make_identity(nc, ident[:])
        for q in range(QUADS):
            nc.gpsimd.dma_start(
                out=tab_sc[QUAD * q:QUAD * q + 4 * K_PASSES, :].bitcast(I32),
                in_=tab_scales[:, 4 * q:4 * q + 4, :].bitcast(I32),
            )
        nc.gpsimd.memset(w2_sc[:].bitcast(I32), 0)
        raw0 = [load_staged(w1, 0, r_cols[0])]
        nc.sync.dma_start(out=wgs_sb[:], in_=wgs)
        raw0.append(load_staged(w1, 1, r_cols[0]))
        nc.sync.dma_start(out=gn[:, :, 0:PACK], in_=gain.rearrange("(b p i) -> p b i", p=P, i=PACK))
        raw0.append(load_staged(w1, 2, r_cols[0]))
        load_table(0)
        nc.sync.dma_start(out=idx[:], in_=offs)
        load_table(1)
        load_table(2)
        nc.sync.dma_start(out=bias[:, :, 0:PACK], in_=b1.rearrange("(b p i) -> p b i", p=P, i=PACK))
        nc.sync.dma_start(out=idx2[:], in_=offs2)
        for i in range(PACK):
            load_page(0, i)
        nc.sync.dma_start(out=idx3[:], in_=offs3)
        deal_wgs()
        raw1 = [load_staged(w1, a, r_cols[1]) for a in range(last)]
        raw1.append(load_pass(keep.tile([P, PACK, PASS], F32, name="raw1_last", tag="middle"), w1, last, r_cols[1]))
        nc.sync.dma_start(out=wgt_sb[:], in_=wgt)
        load_page(1, 0)
        load_pass(att_sb[0], att, 0, slice(0, M))
        for i in range(1, PACK):
            load_page(1, i)
        nc.sync.dma_start(out=w2_wd[:].bitcast(I32), in_=w2_words.rearrange("a p c -> p a c").bitcast(I32))
        for q in range(QUADS):
            nc.sync.dma_start(
                out=w2_sc[QUAD * q:QUAD * q + 4, :, :].bitcast(I32),
                in_=w2_scales[:, 4 * q:4 * q + 4, :].rearrange("a r n -> r a n").bitcast(I32),
            )

        nc.vector.tensor_copy(out=v_sc[:], in_=tab_sc[:].indirect(idx[:]))
        casts = [nc.scalar.copy] * last + [nc.vector.tensor_copy]
        w1q = [quantise_w1(raw0[a], "w1q0_%d" % a, casts[a]) for a in range(K_PASSES)]
        factors0 = scatter_factors(0, keep.tile([P, PACK, S], F32, name="wg0"))
        for a in range(last):
            gather_table(a, 0, S)
            for hs in range(2):
                first_pass(y_bank[hs], a, w1q[a], 0, hs * HALF_S, HALF_S)
            for i in (1, 2):
                first_pass(y_bank[i + 1], a, w1q[a], i, 0, S)
        th_halves = []
        for hs in range(2):
            gather_table(last, hs * HALF_S, HALF_S)
            first_pass(y_bank[hs], last, w1q[last], 0, hs * HALF_S, HALF_S)
            th_halves.append(tanh(0, 0, y_bank[hs], HALF_S))
        th0 = {}
        for i in (1, 2):
            first_pass(y_bank[i + 1], last, w1q[last], i, 0, S)
            th0[i] = tanh(0, i, y_bank[i + 1], S)
        for a in range(K_PASSES):
            first_pass(y_bank[0], a, w1q[a], 3, 0, S)
        th0[3] = tanh(0, 3, y_bank[0], S)
        raw3 = [load_staged(w3, 0, slice(0, N))]
        load_pass(att_sb[1], att, 1, slice(0, M))
        raw3.append(load_pass(late.tile([P, PACK, PASS], F32, name="raw3_last", offset=0, align_bytes=ALIGN), w3, 1, slice(0, N)))
        x0 = keep.tile([P, PACK, M], F32, name="x0")
        for hs in range(2):
            scatter(0, 0, th_halves[hs], factors0, hs * HALF_S, HALF_S)
        for i in range(1, PACK):
            scatter(0, i, th0[i], factors0, 0, S)

        banks1 = [y_bank[(i + 1) % PACK] for i in range(PACK)]
        for a in range(K_PASSES):
            w1q1 = quantise_w1(raw1[a], "w1q1_%d" % a, nc.scalar.copy)
            for i in range(PACK):
                first_pass(banks1[i], a, w1q1, i, 0, S)
        factors1 = scatter_factors(1, keep.tile([P, PACK, S], F32, name="wg1", tag="middle"))
        for i in range(PACK):
            gather(0, i, x0[:], 0, M)
        th1 = [tanh(1, i, banks1[i], S) for i in range(PACK)]
        x0_bf = round_rows(x0[:], M)
        scatter(1, 0, th1[0], factors1, 0, S)
        tilt0_bf = round_rows(tilt_in_place(0, x0[:], 0, M), M)
        scatter(1, 1, th1[1], factors1, 0, S)
        xq0 = quantise_new(x0_bf, M, "xq0")
        scatter(1, 2, th1[2], factors1, 0, S)
        scatter(1, 3, th1[3], factors1, 0, S)
        w3q = [quantise_new(round_rows(raw3[b][:], N), N, "w3q%d" % b) for b in range(H_PASSES)]
        for hf in range(2):
            x_passes(0, hf, xq0, hf * HALF_M)

        half_bytes = PACK * HALF_M * 4
        x1 = [
            late.tile([P, PACK, HALF_M], F32, name="x1_%d" % hf, offset=hf * half_bytes, align_bytes=ALIGN)[:]
            for hf in range(2)
        ]
        for i in range(PACK):
            gather(1, i, x1[0], 0, HALF_M)
        x1_bf0 = round_rows(x1[0], HALF_M)
        gather(1, 0, x1[1], HALF_M, HALF_M)
        tilt1_bf0 = round_rows(tilt_in_place(1, x1[0], 0, HALF_M), HALF_M)
        gather(1, 1, x1[1], HALF_M, HALF_M)
        x_passes(1, 0, quantise_new(x1_bf0, HALF_M, "xq1_0"), 0)
        tq0 = quantise(tilt0_bf, late.tile([P, M], U32, name="tq0_wd", offset=0, align_bytes=ALIGN), "tq0")
        for hf in range(2):
            tilt_passes(0, hf, tq0, hf * HALF_M, w3q[0])
        gather(1, 2, x1[1], HALF_M, HALF_M)
        gather(1, 3, x1[1], HALF_M, HALF_M)
        x1_bf1 = round_rows(x1[1], HALF_M)
        tilt_passes(1, 0, quantise_new(tilt1_bf0, HALF_M, "tq1_0"), 0, w3q[1])
        tilt1_bf1 = tilt_rounded(1, x1[1], HALF_M, HALF_M)
        for g in range(2):
            store(0, g, nc.scalar.copy)
        x_passes(1, 1, quantise_new(x1_bf1, HALF_M, "xq1_1"), 0)
        tilt_passes(1, 1, quantise_new(tilt1_bf1, HALF_M, "tq1_1"), 0, w3q[1])
        store(1, 0, nc.scalar.copy)
        store(1, 1, nc.vector.tensor_copy)
